import numpy as np, ml_dtypes
CORES = [37,45,53,61,69,109,117,125]
N = 8
import mx_ref
NC, WB = 512, 1
D = 2 * WB + 1
BF = ml_dtypes.bfloat16
def setup_inputs(rng):
    def f(*shape):
        return mx_ref.flush((rng.standard_normal(shape, dtype=np.float32) * np.exp2(rng.integers(-2, 3, shape[:-1] + (1,)))).astype(BF))
    return {"w": f(N, 128, 512), "x": f(N, 128, 4 * NC)}
def setup_inputs_blocks(rng):
    d = setup_inputs(rng)
    for k in ("w", "x"): d[k] = mx_ref.spread(d[k], rng, 4)
    return d
def setup_inputs_wide(rng):
    d = setup_inputs(rng)
    for k in ("w", "x"): d[k] = mx_ref.flush((d[k].astype(np.float32) * np.exp2(rng.integers(-8, 9, (N, 1, 1))).astype(np.float32)).astype(BF))
    return d
def setup_inputs_zeros(rng):
    d = setup_inputs(rng); v = d["x"].reshape(N, 128, -1, 4).copy()
    v[np.broadcast_to((rng.random((N, 1, v.shape[2], 1)) < 0.33), v.shape)] = 0
    d["x"] = v.reshape(d["x"].shape)
    return d
def reference(w, x):
    QX = [mx_ref.quantize(x[j]) for j in range(N)]
    y = np.zeros((N, 128, D * NC), np.float32)
    for r in range(N):
        qw = mx_ref.quantize(w[r])
        for i in range(D):
            y[r][:, NC * i:NC * i + NC] = mx_ref.matmul(qw, QX[(r + i - WB) % N])
    return {"y": y}

@@ -1,0 +1,178 @@
+from concourse.bass import DstId, RemoteDMATransfer
+from concourse.mybir import dt, ActivationFunctionType
+
+NC = 512
+MW = 128
+LOADS = ((0, 128), (128, 512))
+CODES = ((0, 128), (128, 512))
+ORDER = ("c0", "p", "c1")
+FAN = 1
+
+PIECE = {"c%d" % i: ("q", a, b) for i, (a, b) in enumerate(CODES)}
+PIECE["p"] = ("s", 0, NC)
+PARTS = tuple("c%d" % i for i in range(len(CODES)))
+SIDES = ("L", "R")
+
+SCRATCH = {
+    "xb": ("sbuf", [128, 4 * NC], "bfloat16"),
+    "wb": ("sbuf", [128, 4 * MW], "bfloat16"),
+    "qx": ("sbuf", [128, NC], "float8_e4m3fn_x4"),
+    "sx": ("sbuf", [128, NC], "uint8"),
+    "qw": ("sbuf", [128, MW], "float8_e4m3fn_x4"),
+    "sw": ("sbuf", [128, MW], "uint8"),
+    "qL": ("sbuf", [128, NC], "float8_e4m3fn_x4"),
+    "sL": ("sbuf", [128, NC], "uint8"),
+    "qR": ("sbuf", [128, NC], "float8_e4m3fn_x4"),
+    "sR": ("sbuf", [128, NC], "uint8"),
+    "ps": ("psum", [128, 512 * (1 + 2 * len(CODES))], "float32"),
+    "ysb": ("sbuf", [128, 3 * NC], "float32"),
+}
+
+SEMAPHORES = (
+    ["ld_w", "q_w", "sent", "mm_own", "cp_own", "st_own"]
+    + ["%s_x%d" % (k, i) for k in ("ld", "q") for i in range(len(LOADS))]
+    + ["a%s_%s" % (s, p) for s in SIDES for p in ORDER]
+    + ["%s_%s%s" % (k, s, p) for k in ("mm", "cp", "st") for s in SIDES for p in PARTS]
+)
+
+
+def _engines(mask):
+    return [1 << b for b in range(mask.bit_length()) if (mask >> b) & 1]
+
+
+def _count(mask):
+    return len(_engines(mask))
+
+
+def _shares(mask, k):
+    bits = _engines(mask)
+    h = len(bits) // k
+    return [sum(bits[i * h:(i + 1) * h]) for i in range(k)]
+
+
+def _relays(topo, T, src, dst, own_die):
+    found = [c for c in range(topo.CHIPS * topo.CORES_PER_CHIP)
+             if topo.chip(c) == topo.chip(src) and T.rank_of(c) is None and topo.may_write(c, dst)
+             and (topo.die(c) == topo.die(src)) == own_die]
+    return found[:FAN]
+
+
+def _flows(topo, T):
+    n = len(T.cores)
+    out = []
+    for j, src in enumerate(T.cores):
+        up, down = T.cores[(j + 1) % n], T.cores[(j - 1) % n]
+        out.append((src, _relays(topo, T, src, up, True), up, "L"))
+        out.append((src, _relays(topo, T, src, down, False), down, "R"))
+    return out
+
+
+def _view(T, where, piece, i):
+    kind, a, b = PIECE[piece]
+    w = (b - a) // FAN
+    ap = T[kind + where][:, a + i * w:a + (i + 1) * w]
+    return ap.bitcast(dt.uint8) if kind == "q" else ap
+
+
+def _slot(side, i):
+    return SIDES.index(side) * FAN + i
+
+
+def _relay_program(g, core, T, topo, src, dst, side, i):
+    share = _count(_shares(topo.mask(src, core), 2 * FAN)[_slot(side, i)])
+    rid, pid, _ = topo.addr(dst)
+    mask = topo.mask(core, dst)
+    for piece in ORDER:
+        sem = T.sem["a%s_%s" % (side, piece)]
+        v = _view(T, side, piece, i)
+        g.wait_ge(sem, share)
+        g.remote_dma(out_ap=v, in_ap=v, remote_sem=sem, local_sem=T.sem.sent, pid=pid, routing_id=rid,
+                     dma_engine_mask=mask)
+    g.wait_ge(T.sem.sent, len(ORDER) * _count(mask))
+
+
+def rank_program(g, core, T, topo):
+    flows = _flows(topo, T)
+    rank = T.rank_of(core)
+    if rank is None:
+        for src, relays, dst, side in flows:
+            if core in relays:
+                _relay_program(g, core, T, topo, src, dst, side, relays.index(core))
+        return
+
+    S = T.sem
+    v = g.vector
+    t = g.tensor
+    for i, (a, b) in enumerate(LOADS):
+        g.sync.dma_start(T.xb[:, 4 * a:4 * b], T.x[:, 4 * a:4 * b]).then_inc(S["ld_x%d" % i], 16)
+    g.sync.dma_start(T.wb[:], T.w[:]).then_inc(S.ld_w, 16)
+    for i, (a, b) in enumerate(LOADS):
+        v.wait_ge(S["ld_x%d" % i], 16)
+        v.quantize_mx(T.qx[:, a:b], T.sx[:, a:b], T.xb[:, 4 * a:4 * b]).then_inc(S["q_x%d" % i], 1)
+    v.wait_ge(S.ld_w, 16)
+    v.quantize_mx(T.qw[:], T.sw[:], T.wb[:]).then_inc(S.q_w, 1)
+
+    mine = [f for f in flows if f[0] == core]
+    sent = 0
+    seen = set()
+    for piece in ORDER:
+        _, a, b = PIECE[piece]
+        for i, (la, lb) in enumerate(LOADS):
+            if la < b and a < lb and i not in seen:
+                seen.add(i)
+                g.wait_ge(S["q_x%d" % i], 1)
+        transfers = []
+        for _, relays, _, side in mine:
+            for i, relay in enumerate(relays):
+                rid, pid, _ = topo.addr(relay)
+                m = _shares(topo.mask(core, relay), 2 * FAN)[_slot(side, i)]
+                sent += _count(m)
+                transfers.append(RemoteDMATransfer(
+                    dst_ids=[DstId(rid=rid, pnc=pid)], dma_engine_mask=m, remote_sem=S["a%s_%s" % (side, piece)],
+                    src=_view(T, "x", piece, i), dst=_view(T, side, piece, i)))
+        g.remote_dma_fused(transfers, local_sem=S.sent)
+
+    coming = {side: (src, relays) for src, relays, dst, side in flows if dst == core}
+    order = sorted(SIDES, key=lambda s: 0 if topo.mates(topo.chip(coming[s][0]), topo.chip(core)) else 1)
+    got = {s: sum(_count(topo.mask(r, core)) for r in coming[s][1]) for s in SIDES}
+    bank = {s + p: 1 + len(PARTS) * SIDES.index(s) + PARTS.index(p) for s in SIDES for p in PARTS}
+    block = {"L": 0, "own": 1, "R": 2}
+    t.wait_ge(S.q_w, 1)
+    for i in range(len(LOADS)):
+        t.wait_ge(S["q_x%d" % i], 1)
+    t.matmul_mx(T.ps[:, 0:NC], T.qw[:], T.sw[:], T.qx[:], T.sx[:], True, True).then_inc(S.mm_own, 1)
+    for part in PARTS:
+        _, a, b = PIECE[part]
+        for s in order:
+            if part == PARTS[0]:
+                t.wait_ge(S["a%s_p" % s], got[s])
+            t.wait_ge(S["a%s_%s" % (s, part)], got[s])
+            o = 512 * bank[s + part]
+            t.matmul_mx(T.ps[:, o:o + b - a], T.qw[:], T.sw[:], T["q" + s][:, a:b], T["s" + s][:, a:b],
+                        True, True).then_inc(S["mm_%s%s" % (s, part)], 1)
+
+    o = NC * block["own"]
+    v.wait_ge(S.mm_own, 1)
+    v.tensor_copy(T.ysb[:, o:o + NC], T.ps[:, 0:NC]).then_inc(S.cp_own, 1)
+    g.sync.wait_ge(S.cp_own, 1)
+    g.sync.wait_ge(S.sent, sent)
+    g.sync.dma_start(T.y[:, o:o + NC], T.ysb[:, o:o + NC]).then_inc(S.st_own, 16)
+    for part in PARTS:
+        _, a, b = PIECE[part]
+        for s, q in (("L", g.sync), ("R", g.scalar)):
+            k = s + part
+            o = NC * block[s]
+            p = 512 * bank[k]
+            if s == "L":
+                v.wait_ge(S["mm_" + k], 1)
+                v.tensor_copy(T.ysb[:, o + a:o + b], T.ps[:, p:p + b - a]).then_inc(S["cp_" + k], 1)
+            else:
+                q.wait_ge(S["mm_" + k], 1)
+                q.activation(T.ysb[:, o + a:o + b], T.ps[:, p:p + b - a],
+                             ActivationFunctionType.Copy).then_inc(S["cp_" + k], 1)
+            q.wait_ge(S["cp_" + k], 1)
+            q.dma_start(T.y[:, o + a:o + b], T.ysb[:, o + a:o + b]).then_inc(S["st_" + k], 16)
+    g.sync.wait_ge(S.st_own, 16)
+    for part in PARTS:
+        g.sync.wait_ge(S["st_L" + part], 16)
+        g.scalar.wait_ge(S["st_R" + part], 16)

@@ -4,8 +4,8 @@ from concourse.mybir import dt, ActivationFunctionType
 NC = 512
 MW = 128
 LOADS = ((0, 128), (128, 512))
-CODES = ((0, 128), (128, 512))
-ORDER = ("c0", "p", "c1")
+CODES = ((0, 128), (128, 384), (384, 512))
+ORDER = ("c0", "p", "c1", "c2")
 FAN = 1
 
 PIECE = {"c%d" % i: ("q", a, b) for i, (a, b) in enumerate(CODES)}

from concourse.bass import DstId, RemoteDMATransfer
from concourse.mybir import dt, ActivationFunctionType

NC = 512
MW = 128
LOADS = ((0, 128), (128, 512))
CODES = ((0, 128), (128, 384), (384, 512))
ORDER = ("c0", "p", "c1", "c2")
FAN = 1

PIECE = {"c%d" % i: ("q", a, b) for i, (a, b) in enumerate(CODES)}
PIECE["p"] = ("s", 0, NC)
PARTS = tuple("c%d" % i for i in range(len(CODES)))
SIDES = ("L", "R")

SCRATCH = {
    "xb": ("sbuf", [128, 4 * NC], "bfloat16"),
    "wb": ("sbuf", [128, 4 * MW], "bfloat16"),
    "qx": ("sbuf", [128, NC], "float8_e4m3fn_x4"),
    "sx": ("sbuf", [128, NC], "uint8"),
    "qw": ("sbuf", [128, MW], "float8_e4m3fn_x4"),
    "sw": ("sbuf", [128, MW], "uint8"),
    "qL": ("sbuf", [128, NC], "float8_e4m3fn_x4"),
    "sL": ("sbuf", [128, NC], "uint8"),
    "qR": ("sbuf", [128, NC], "float8_e4m3fn_x4"),
    "sR": ("sbuf", [128, NC], "uint8"),
    "ps": ("psum", [128, 512 * (1 + 2 * len(CODES))], "float32"),
    "ysb": ("sbuf", [128, 3 * NC], "float32"),
}

SEMAPHORES = (
    ["ld_w", "q_w", "sent", "mm_own", "cp_own", "st_own"]
    + ["%s_x%d" % (k, i) for k in ("ld", "q") for i in range(len(LOADS))]
    + ["a%s_%s" % (s, p) for s in SIDES for p in ORDER]
    + ["%s_%s%s" % (k, s, p) for k in ("mm", "cp", "st") for s in SIDES for p in PARTS]
)


def _engines(mask):
    return [1 << b for b in range(mask.bit_length()) if (mask >> b) & 1]


def _count(mask):
    return len(_engines(mask))


def _shares(mask, k):
    bits = _engines(mask)
    h = len(bits) // k
    return [sum(bits[i * h:(i + 1) * h]) for i in range(k)]


def _relays(topo, T, src, dst, own_die):
    found = [c for c in range(topo.CHIPS * topo.CORES_PER_CHIP)
             if topo.chip(c) == topo.chip(src) and T.rank_of(c) is None and topo.may_write(c, dst)
             and (topo.die(c) == topo.die(src)) == own_die]
    return found[:FAN]


def _flows(topo, T):
    n = len(T.cores)
    out = []
    for j, src in enumerate(T.cores):
        up, down = T.cores[(j + 1) % n], T.cores[(j - 1) % n]
        out.append((src, _relays(topo, T, src, up, True), up, "L"))
        out.append((src, _relays(topo, T, src, down, False), down, "R"))
    return out


def _view(T, where, piece, i):
    kind, a, b = PIECE[piece]
    w = (b - a) // FAN
    ap = T[kind + where][:, a + i * w:a + (i + 1) * w]
    return ap.bitcast(dt.uint8) if kind == "q" else ap


def _slot(side, i):
    return SIDES.index(side) * FAN + i


def _relay_program(g, core, T, topo, src, dst, side, i):
    share = _count(_shares(topo.mask(src, core), 2 * FAN)[_slot(side, i)])
    rid, pid, _ = topo.addr(dst)
    mask = topo.mask(core, dst)
    for piece in ORDER:
        sem = T.sem["a%s_%s" % (side, piece)]
        v = _view(T, side, piece, i)
        g.wait_ge(sem, share)
        g.remote_dma(out_ap=v, in_ap=v, remote_sem=sem, local_sem=T.sem.sent, pid=pid, routing_id=rid,
                     dma_engine_mask=mask)
    g.wait_ge(T.sem.sent, len(ORDER) * _count(mask))


def rank_program(g, core, T, topo):
    flows = _flows(topo, T)
    rank = T.rank_of(core)
    if rank is None:
        for src, relays, dst, side in flows:
            if core in relays:
                _relay_program(g, core, T, topo, src, dst, side, relays.index(core))
        return

    S = T.sem
    v = g.vector
    t = g.tensor
    for i, (a, b) in enumerate(LOADS):
        g.sync.dma_start(T.xb[:, 4 * a:4 * b], T.x[:, 4 * a:4 * b]).then_inc(S["ld_x%d" % i], 16)
    g.sync.dma_start(T.wb[:], T.w[:]).then_inc(S.ld_w, 16)
    for i, (a, b) in enumerate(LOADS):
        v.wait_ge(S["ld_x%d" % i], 16)
        v.quantize_mx(T.qx[:, a:b], T.sx[:, a:b], T.xb[:, 4 * a:4 * b]).then_inc(S["q_x%d" % i], 1)
    v.wait_ge(S.ld_w, 16)
    v.quantize_mx(T.qw[:], T.sw[:], T.wb[:]).then_inc(S.q_w, 1)

    mine = [f for f in flows if f[0] == core]
    sent = 0
    seen = set()
    for piece in ORDER:
        _, a, b = PIECE[piece]
        for i, (la, lb) in enumerate(LOADS):
            if la < b and a < lb and i not in seen:
                seen.add(i)
                g.wait_ge(S["q_x%d" % i], 1)
        transfers = []
        for _, relays, _, side in mine:
            for i, relay in enumerate(relays):
                rid, pid, _ = topo.addr(relay)
                m = _shares(topo.mask(core, relay), 2 * FAN)[_slot(side, i)]
                sent += _count(m)
                transfers.append(RemoteDMATransfer(
                    dst_ids=[DstId(rid=rid, pnc=pid)], dma_engine_mask=m, remote_sem=S["a%s_%s" % (side, piece)],
                    src=_view(T, "x", piece, i), dst=_view(T, side, piece, i)))
        g.remote_dma_fused(transfers, local_sem=S.sent)

    coming = {side: (src, relays) for src, relays, dst, side in flows if dst == core}
    order = sorted(SIDES, key=lambda s: 0 if topo.mates(topo.chip(coming[s][0]), topo.chip(core)) else 1)
    got = {s: sum(_count(topo.mask(r, core)) for r in coming[s][1]) for s in SIDES}
    bank = {s + p: 1 + len(PARTS) * SIDES.index(s) + PARTS.index(p) for s in SIDES for p in PARTS}
    block = {"L": 0, "own": 1, "R": 2}
    t.wait_ge(S.q_w, 1)
    for i in range(len(LOADS)):
        t.wait_ge(S["q_x%d" % i], 1)
    t.matmul_mx(T.ps[:, 0:NC], T.qw[:], T.sw[:], T.qx[:], T.sx[:], True, True).then_inc(S.mm_own, 1)
    for part in PARTS:
        _, a, b = PIECE[part]
        for s in order:
            if part == PARTS[0]:
                t.wait_ge(S["a%s_p" % s], got[s])
            t.wait_ge(S["a%s_%s" % (s, part)], got[s])
            o = 512 * bank[s + part]
            t.matmul_mx(T.ps[:, o:o + b - a], T.qw[:], T.sw[:], T["q" + s][:, a:b], T["s" + s][:, a:b],
                        True, True).then_inc(S["mm_%s%s" % (s, part)], 1)

    o = NC * block["own"]
    v.wait_ge(S.mm_own, 1)
    v.tensor_copy(T.ysb[:, o:o + NC], T.ps[:, 0:NC]).then_inc(S.cp_own, 1)
    g.sync.wait_ge(S.cp_own, 1)
    g.sync.wait_ge(S.sent, sent)
    g.sync.dma_start(T.y[:, o:o + NC], T.ysb[:, o:o + NC]).then_inc(S.st_own, 16)
    for part in PARTS:
        _, a, b = PIECE[part]
        for s, q in (("L", g.sync), ("R", g.scalar)):
            k = s + part
            o = NC * block[s]
            p = 512 * bank[k]
            if s == "L":
                v.wait_ge(S["mm_" + k], 1)
                v.tensor_copy(T.ysb[:, o + a:o + b], T.ps[:, p:p + b - a]).then_inc(S["cp_" + k], 1)
            else:
                q.wait_ge(S["mm_" + k], 1)
                q.activation(T.ysb[:, o + a:o + b], T.ps[:, p:p + b - a],
                             ActivationFunctionType.Copy).then_inc(S["cp_" + k], 1)
            q.wait_ge(S["cp_" + k], 1)
            q.dma_start(T.y[:, o + a:o + b], T.ysb[:, o + a:o + b]).then_inc(S["st_" + k], 16)
    g.sync.wait_ge(S.st_own, 16)
    for part in PARTS:
        g.sync.wait_ge(S["st_L" + part], 16)
        g.scalar.wait_ge(S["st_R" + part], 16)
